import numpy as np
import ml_dtypes

BF16 = ml_dtypes.bfloat16


def bf(x):
    return np.asarray(x, np.float32).astype(BF16)


def f32(x):
    return np.asarray(x, np.float32)


def f64(x):
    return np.asarray(x).astype(np.float64)


def striped(idx):
    return np.concatenate([l.reshape(-1, 16).T for l in idx])


def rows(idx, k):
    return np.tile(np.repeat(idx, 16, axis=0), (k // (16 * 8), 1))


def look(tab, idx):
    return np.take_along_axis(f64(tab), rows(idx, len(tab)), axis=1)


K, S, V, N, M = 128, 2048, 2048, 2048, 256


def silu(v):
    return v / (1.0 + np.exp(-v))


def setup_inputs():
    return {"tab": f32(np.random.standard_normal((2, K, S))), "w": bf(np.random.standard_normal((K, M)) / np.sqrt(K)), "b": f32(0.5 * np.random.standard_normal((M, 1))), "offs": striped(np.stack([np.random.permutation(S)[:N] for _ in range(8)]))}


def reference(tab, w, b, offs):
    idx = np.stack([g.T.reshape(-1) for g in np.split(offs, 8)])
    x = ((look(tab[0], idx) - 0.125) * 1.5) * (silu(look(tab[1], idx)))
    return np.maximum(f64(w).T @ x + f64(b), 0.0)

@@ -1,0 +1,57 @@
+import concourse.mybir as mybir
+
+BF16, F32, U16 = mybir.dt.bfloat16, mybir.dt.float32, mybir.dt.uint16
+ALU = mybir.AluOpType
+SILU = mybir.ActivationFunctionType.Silu
+RELU = mybir.ActivationFunctionType.Relu
+
+K, S, N, M = 128, 2048, 2048, 256
+P = 128
+PIECE = 512
+SHIFT, SCALE = 0.125, 1.5
+
+FLOPS = 2 * K * M * N
+
+
+def tile_lookup_vg_nrmsilu_relu_kernel(tc, tab, w, b, offs, out):
+    nc = tc.nc
+    blocks = M // P
+    with (
+        tc.tile_pool(name="held", bufs=1) as held,
+        tc.tile_pool(name="work", bufs=2) as work,
+        tc.tile_pool(name="results", bufs=4) as results,
+        tc.psum_pool(name="psum", bufs=4) as psum,
+    ):
+        lists = held.tile([P, N // 16], U16, name="lists")
+        values = held.tile([P, S], F32, name="values")
+        gates = held.tile([P, S], F32, name="gates")
+        weights = held.tile([K, M], BF16, name="weights")
+        biases = [held.tile([P, 1], F32, name=f"bias{block}") for block in range(blocks)]
+
+        nc.sync.dma_start(lists[:], offs)
+        nc.sync.dma_start(values[:], tab[0])
+        nc.sync.dma_start(gates[:], tab[1])
+        nc.gpsimd.dma_start(weights[:], w)
+        for block in range(blocks):
+            nc.gpsimd.dma_start(biases[block][:], b[block * P : (block + 1) * P, :])
+
+        for start in range(0, N, PIECE):
+            piece = lists[:, start // 16 : (start + PIECE) // 16]
+
+            value = work.tile([P, PIECE], F32, name="value")
+            nc.vector.tensor_scalar(value[:], values[:].indirect(piece), SHIFT, SCALE, ALU.subtract, ALU.mult)
+            gate = work.tile([P, PIECE], F32, name="gate")
+            nc.scalar.activation(gate[:], gates[:].indirect(piece), SILU)
+            x = work.tile([P, PIECE], BF16, name="x")
+            nc.vector.tensor_tensor(x[:], value[:], gate[:], ALU.mult)
+
+            for block in range(blocks):
+                rows = slice(block * P, (block + 1) * P)
+                product = psum.tile([P, PIECE], F32, name="product")
+                nc.tensor.matmul(product[:], weights[:, rows], x[:], start=True, stop=True)
+                result = results.tile([P, PIECE], F32, name="result")
+                if block % 2 == 0:
+                    nc.scalar.activation(result[:], product[:], RELU, bias=biases[block][:])
+                else:
+                    nc.vector.tensor_scalar(result[:], product[:], biases[block][:], 0.0, ALU.add, ALU.max)
+                nc.sync.dma_start(out[rows, start : start + PIECE], result[:])

@@ -18,9 +18,9 @@ def tile_lookup_vg_nrmsilu_relu_kernel(tc, tab, w, b, offs, out):
     blocks = M // P
     with (
         tc.tile_pool(name="held", bufs=1) as held,
-        tc.tile_pool(name="work", bufs=2) as work,
-        tc.tile_pool(name="results", bufs=4) as results,
-        tc.psum_pool(name="psum", bufs=4) as psum,
+        tc.tile_pool(name="work", bufs=N // PIECE) as work,
+        tc.tile_pool(name="results", bufs=8) as results,
+        tc.psum_pool(name="psum", bufs=8) as psum,
     ):
         lists = held.tile([P, N // 16], U16, name="lists")
         values = held.tile([P, S], F32, name="values")

@@ -35,6 +35,10 @@ def tile_lookup_vg_nrmsilu_relu_kernel(tc, tab, w, b, offs, out):
         for block in range(blocks):
             nc.gpsimd.dma_start(biases[block][:], b[block * P : (block + 1) * P, :])
 
+        warm = held.tile([P, 2], F32, name="warm")
+        nc.vector.memset(warm[:, 0:1], 0.0)
+        nc.scalar.activation(warm[:, 1:2], warm[:, 0:1], SILU)
+
         for start in range(0, N, PIECE):
             piece = lists[:, start // 16 : (start + PIECE) // 16]
 

@@ -10,6 +10,8 @@ P = 128
 PIECE = 512
 SHIFT, SCALE = 0.125, 1.5
 
+WARM_MATMULS = 24
+
 FLOPS = 2 * K * M * N
 
 
@@ -18,9 +20,12 @@ def tile_lookup_vg_nrmsilu_relu_kernel(tc, tab, w, b, offs, out):
     blocks = M // P
     with (
         tc.tile_pool(name="held", bufs=1) as held,
+        tc.tile_pool(name="ahead", bufs=3) as ahead,
+        tc.tile_pool(name="gated", bufs=2) as gated,
         tc.tile_pool(name="work", bufs=N // PIECE) as work,
         tc.tile_pool(name="results", bufs=8) as results,
-        tc.psum_pool(name="psum", bufs=8) as psum,
+        tc.psum_pool(name="psum", bufs=7) as psum,
+        tc.psum_pool(name="unread_bank", bufs=1) as unread_bank,
     ):
         lists = held.tile([P, N // 16], U16, name="lists")
         values = held.tile([P, S], F32, name="values")
@@ -39,12 +44,18 @@ def tile_lookup_vg_nrmsilu_relu_kernel(tc, tab, w, b, offs, out):
         nc.vector.memset(warm[:, 0:1], 0.0)
         nc.scalar.activation(warm[:, 1:2], warm[:, 0:1], SILU)
 
+        zeros = held.tile([P, PIECE], BF16, name="zeros")
+        nc.vector.memset(zeros[:], 0.0)
+        unread = unread_bank.tile([P, PIECE], F32, name="unread")
+        for repeat in range(WARM_MATMULS):
+            nc.tensor.matmul(unread[:], zeros[:, 0:P], zeros[:], start=True, stop=True)
+
         for start in range(0, N, PIECE):
             piece = lists[:, start // 16 : (start + PIECE) // 16]
 
-            value = work.tile([P, PIECE], F32, name="value")
+            value = ahead.tile([P, PIECE], F32, name="value")
             nc.vector.tensor_scalar(value[:], values[:].indirect(piece), SHIFT, SCALE, ALU.subtract, ALU.mult)
-            gate = work.tile([P, PIECE], F32, name="gate")
+            gate = gated.tile([P, PIECE], F32, name="gate")
             nc.scalar.activation(gate[:], gates[:].indirect(piece), SILU)
             x = work.tile([P, PIECE], BF16, name="x")
             nc.vector.tensor_tensor(x[:], value[:], gate[:], ALU.mult)

@@ -36,9 +36,9 @@ def tile_lookup_vg_nrmsilu_relu_kernel(tc, tab, w, b, offs, out):
         nc.sync.dma_start(lists[:], offs)
         nc.sync.dma_start(values[:], tab[0])
         nc.sync.dma_start(gates[:], tab[1])
-        nc.gpsimd.dma_start(weights[:], w)
+        nc.sync.dma_start(weights[:], w)
         for block in range(blocks):
-            nc.gpsimd.dma_start(biases[block][:], b[block * P : (block + 1) * P, :])
+            nc.sync.dma_start(biases[block][:], b[block * P : (block + 1) * P, :])
 
         warm = held.tile([P, 2], F32, name="warm")
         nc.vector.memset(warm[:, 0:1], 0.0)

import concourse.mybir as mybir

BF16, F32, U16 = mybir.dt.bfloat16, mybir.dt.float32, mybir.dt.uint16
ALU = mybir.AluOpType
SILU = mybir.ActivationFunctionType.Silu
RELU = mybir.ActivationFunctionType.Relu

K, S, N, M = 128, 2048, 2048, 256
P = 128
PIECE = 512
SHIFT, SCALE = 0.125, 1.5

WARM_MATMULS = 24

FLOPS = 2 * K * M * N


def tile_lookup_vg_nrmsilu_relu_kernel(tc, tab, w, b, offs, out):
    nc = tc.nc
    blocks = M // P
    with (
        tc.tile_pool(name="held", bufs=1) as held,
        tc.tile_pool(name="ahead", bufs=3) as ahead,
        tc.tile_pool(name="gated", bufs=2) as gated,
        tc.tile_pool(name="work", bufs=N // PIECE) as work,
        tc.tile_pool(name="results", bufs=8) as results,
        tc.psum_pool(name="psum", bufs=7) as psum,
        tc.psum_pool(name="unread_bank", bufs=1) as unread_bank,
    ):
        lists = held.tile([P, N // 16], U16, name="lists")
        values = held.tile([P, S], F32, name="values")
        gates = held.tile([P, S], F32, name="gates")
        weights = held.tile([K, M], BF16, name="weights")
        biases = [held.tile([P, 1], F32, name=f"bias{block}") for block in range(blocks)]

        nc.sync.dma_start(lists[:], offs)
        nc.sync.dma_start(values[:], tab[0])
        nc.sync.dma_start(gates[:], tab[1])
        nc.sync.dma_start(weights[:], w)
        for block in range(blocks):
            nc.sync.dma_start(biases[block][:], b[block * P : (block + 1) * P, :])

        warm = held.tile([P, 2], F32, name="warm")
        nc.vector.memset(warm[:, 0:1], 0.0)
        nc.scalar.activation(warm[:, 1:2], warm[:, 0:1], SILU)

        zeros = held.tile([P, PIECE], BF16, name="zeros")
        nc.vector.memset(zeros[:], 0.0)
        unread = unread_bank.tile([P, PIECE], F32, name="unread")
        for repeat in range(WARM_MATMULS):
            nc.tensor.matmul(unread[:], zeros[:, 0:P], zeros[:], start=True, stop=True)

        for start in range(0, N, PIECE):
            piece = lists[:, start // 16 : (start + PIECE) // 16]

            value = ahead.tile([P, PIECE], F32, name="value")
            nc.vector.tensor_scalar(value[:], values[:].indirect(piece), SHIFT, SCALE, ALU.subtract, ALU.mult)
            gate = gated.tile([P, PIECE], F32, name="gate")
            nc.scalar.activation(gate[:], gates[:].indirect(piece), SILU)
            x = work.tile([P, PIECE], BF16, name="x")
            nc.vector.tensor_tensor(x[:], value[:], gate[:], ALU.mult)

            for block in range(blocks):
                rows = slice(block * P, (block + 1) * P)
                product = psum.tile([P, PIECE], F32, name="product")
                nc.tensor.matmul(product[:], weights[:, rows], x[:], start=True, stop=True)
                result = results.tile([P, PIECE], F32, name="result")
                if block % 2 == 0:
                    nc.scalar.activation(result[:], product[:], RELU, bias=biases[block][:])
                else:
                    nc.vector.tensor_scalar(result[:], product[:], biases[block][:], 0.0, ALU.add, ALU.max)
                nc.sync.dma_start(out[rows, start : start + PIECE], result[:])
